import numpy as np
import ml_dtypes

BF16 = ml_dtypes.bfloat16


def bf(x):
    return np.asarray(x, np.float32).astype(BF16)


def f32(x):
    return np.asarray(x, np.float32)


def f64(x):
    return np.asarray(x).astype(np.float64)


def striped(idx):
    return np.tile(idx.reshape(-1, 16).T, (8, 1))


def rows(idx, k):
    return np.tile(idx, (k, 1))


def look(tab, idx):
    return np.take_along_axis(f64(tab), rows(idx, len(tab)), axis=1)


K, S, V, N, M = 128, 256, 256, 256, 128


def setup_inputs():
    return {"tab": f32(np.random.standard_normal((K, S))), "w": bf(np.random.standard_normal((K, M)) / np.sqrt(K)), "b": f32(0.5 * np.random.standard_normal((M, 1))), "offs": striped(np.random.randint(0, S, N))}


def reference(tab, w, b, offs):
    idx = offs[:16].T.reshape(-1)
    t = look(tab, idx)
    x = np.minimum(np.maximum(t, -1.25), 1.0)
    y = f64(w).T @ x
    return np.maximum(y + f64(b), 0.0)

@@ -1,0 +1,41 @@
+import concourse.mybir as mybir
+
+F32 = mybir.dt.float32
+BF16 = mybir.dt.bfloat16
+U16 = mybir.dt.uint16
+ALU = mybir.AluOpType
+ACT = mybir.ActivationFunctionType
+
+R, S, N, M = 128, 256, 256, 128
+LOW, HIGH = -1.25, 1.0
+PIECE = N // 2
+FLOPS = 2 * R * M * N
+
+
+def tile_lookup_deq_clip_relu_kernel(tc, tab, w, b, offs, out):
+    nc = tc.nc
+    with (
+        tc.tile_pool(name="held", bufs=1) as held,
+        tc.tile_pool(name="work", bufs=2) as work,
+        tc.psum_pool(name="psum", bufs=2) as psum,
+    ):
+        offsets = held.tile([128, N // 16], U16)
+        table = held.tile([R, S], F32)
+        weights = held.tile([R, M], BF16)
+        weights_f32 = held.tile([R, M], F32)
+        bias = held.tile([M, 1], F32)
+        nc.sync.dma_start(offsets[:], offs)
+        nc.scalar.dma_start(table[:], tab)
+        nc.sync.dma_start(weights[:], w)
+        nc.scalar.dma_start(bias[:], b)
+        nc.scalar.copy(weights_f32[:], weights[:])
+
+        for first in range(0, N, PIECE):
+            entries = offsets[:, first // 16 : (first + PIECE) // 16]
+            x = work.tile([R, PIECE], F32)
+            nc.vector.tensor_scalar(x[:], table[:].indirect(entries), LOW, HIGH, op0=ALU.max, op1=ALU.min)
+            product = psum.tile([M, PIECE], F32)
+            nc.tensor.matmul(product[:], weights_f32[:], x[:], start=True, stop=True)
+            y = work.tile([M, PIECE], F32)
+            nc.scalar.activation(y[:], product[:], ACT.Relu, bias=bias[:])
+            nc.sync.dma_start(out[:, first : first + PIECE], y[:])

@@ -22,20 +22,20 @@ def tile_lookup_deq_clip_relu_kernel(tc, tab, w, b, offs, out):
         offsets = held.tile([128, N // 16], U16)
         table = held.tile([R, S], F32)
         weights = held.tile([R, M], BF16)
-        weights_f32 = held.tile([R, M], F32)
         bias = held.tile([M, 1], F32)
         nc.sync.dma_start(offsets[:], offs)
         nc.scalar.dma_start(table[:], tab)
         nc.sync.dma_start(weights[:], w)
         nc.scalar.dma_start(bias[:], b)
-        nc.scalar.copy(weights_f32[:], weights[:])
 
         for first in range(0, N, PIECE):
             entries = offsets[:, first // 16 : (first + PIECE) // 16]
             x = work.tile([R, PIECE], F32)
             nc.vector.tensor_scalar(x[:], table[:].indirect(entries), LOW, HIGH, op0=ALU.max, op1=ALU.min)
+            x_bf16 = work.tile([R, PIECE], BF16)
+            nc.vector.tensor_copy(x_bf16[:], x[:])
             product = psum.tile([M, PIECE], F32)
-            nc.tensor.matmul(product[:], weights_f32[:], x[:], start=True, stop=True)
+            nc.tensor.matmul(product[:], weights[:], x_bf16[:], start=True, stop=True)
             y = work.tile([M, PIECE], F32)
             nc.scalar.activation(y[:], product[:], ACT.Relu, bias=bias[:])
             nc.sync.dma_start(out[:, first : first + PIECE], y[:])

@@ -4,7 +4,6 @@ F32 = mybir.dt.float32
 BF16 = mybir.dt.bfloat16
 U16 = mybir.dt.uint16
 ALU = mybir.AluOpType
-ACT = mybir.ActivationFunctionType
 
 R, S, N, M = 128, 256, 256, 128
 LOW, HIGH = -1.25, 1.0
@@ -37,5 +36,5 @@ def tile_lookup_deq_clip_relu_kernel(tc, tab, w, b, offs, out):
             product = psum.tile([M, PIECE], F32)
             nc.tensor.matmul(product[:], weights[:], x_bf16[:], start=True, stop=True)
             y = work.tile([M, PIECE], F32)
-            nc.scalar.activation(y[:], product[:], ACT.Relu, bias=bias[:])
+            nc.vector.tensor_scalar(y[:], product[:], bias[:], 0.0, op0=ALU.add, op1=ALU.max)
             nc.sync.dma_start(out[:, first : first + PIECE], y[:])

import concourse.mybir as mybir

F32 = mybir.dt.float32
BF16 = mybir.dt.bfloat16
U16 = mybir.dt.uint16
ALU = mybir.AluOpType

R, S, N, M = 128, 256, 256, 128
LOW, HIGH = -1.25, 1.0
PIECE = N // 2
FLOPS = 2 * R * M * N


def tile_lookup_deq_clip_relu_kernel(tc, tab, w, b, offs, out):
    nc = tc.nc
    with (
        tc.tile_pool(name="held", bufs=1) as held,
        tc.tile_pool(name="work", bufs=2) as work,
        tc.psum_pool(name="psum", bufs=2) as psum,
    ):
        offsets = held.tile([128, N // 16], U16)
        table = held.tile([R, S], F32)
        weights = held.tile([R, M], BF16)
        bias = held.tile([M, 1], F32)
        nc.sync.dma_start(offsets[:], offs)
        nc.scalar.dma_start(table[:], tab)
        nc.sync.dma_start(weights[:], w)
        nc.scalar.dma_start(bias[:], b)

        for first in range(0, N, PIECE):
            entries = offsets[:, first // 16 : (first + PIECE) // 16]
            x = work.tile([R, PIECE], F32)
            nc.vector.tensor_scalar(x[:], table[:].indirect(entries), LOW, HIGH, op0=ALU.max, op1=ALU.min)
            x_bf16 = work.tile([R, PIECE], BF16)
            nc.vector.tensor_copy(x_bf16[:], x[:])
            product = psum.tile([M, PIECE], F32)
            nc.tensor.matmul(product[:], weights[:], x_bf16[:], start=True, stop=True)
            y = work.tile([M, PIECE], F32)
            nc.vector.tensor_scalar(y[:], product[:], bias[:], 0.0, op0=ALU.add, op1=ALU.max)
            nc.sync.dma_start(out[:, first : first + PIECE], y[:])
